import numpy as np
import ml_dtypes


def mxq(x, axis, fmt="e4m3"):
    dtype, down = {"e4m3": (ml_dtypes.float8_e4m3fn, 7), "e5m2": (ml_dtypes.float8_e5m2, 14)}[fmt]
    v = np.moveaxis(np.asarray(x, np.float32).astype(ml_dtypes.bfloat16).astype(np.float64), axis, -1)
    blocks = v.reshape(v.shape[:-1] + (-1, 32))
    amax = np.abs(blocks).max(-1, keepdims=True)
    byte = np.maximum(np.where(amax > 0, np.frexp(amax)[1] - 1 + 127, 0) - down, 1)
    scale = np.exp2(byte - 127.0)
    codes = (blocks / scale).astype(np.float32).astype(dtype).astype(np.float64)
    return np.moveaxis((codes * scale).reshape(v.shape), -1, axis)


WIDE = False


def mx_kscale(k):
    if not WIDE:
        return np.ones(k)
    levels = np.array([10, -10, 5, -5, 0])
    if k % 512:
        return np.exp2(np.random.permutation(np.resize(levels, k // 32))).repeat(32)
    a = np.empty((k // 512, 16))
    for p in range(k // 512):
        a[p, :8] = np.random.permutation(np.resize(levels, 8))
        for g in range(8):
            far = levels[np.abs(levels - a[p, g]) >= 10]
            a[p, g + 8] = far[np.random.randint(len(far))]
    return np.exp2(a.ravel()).repeat(32)


BF16 = ml_dtypes.bfloat16


def bf(x):
    return np.asarray(x, np.float32).astype(BF16)


def f64(x):
    return np.asarray(x).astype(np.float64)


N, L, F, H, P = 4096, 512, 512, 256, 4
PH = P * H


def draw0():
    s, t = mx_kscale(L), mx_kscale(F)
    return {
        "x": bf(np.random.standard_normal((N, L)) * s),
        "fut": bf(np.random.standard_normal((N, P, H))),
        "w1": bf(np.random.standard_normal((L, F)) / np.sqrt(L) / s[:, None] * t),
        "w2": bf(np.random.standard_normal((F, PH)) * 1.4 / np.sqrt(F) / t[:, None]),
        "wsk": bf(np.random.standard_normal((L, PH)) / np.sqrt(L) / s[:, None]),
        "vp": bf(np.random.uniform(0.4, 0.8, P)),
        "wres": bf(np.random.standard_normal((L, H)) / np.sqrt(L) / s[:, None]),
    }


def residual_block(xq, w1, w2, wsk):
    h = np.maximum(xq @ mxq(f64(w1), 0, "e4m3"), 0.0)
    return (mxq(h, 1, "e4m3") @ mxq(f64(w2), 0, "e4m3")) + (xq @ mxq(f64(wsk), 0, "e4m3"))


def temporal_decoder(g, fut, vp):
    u = np.maximum(g + f64(fut), 0.0)
    return np.sum(f64(vp)[None, :, None] * u, axis=1)


def core(x, fut, w1, w2, wsk, vp, wres):
    xq = mxq(f64(x), 1, "e4m3")
    r = residual_block(xq, w1, w2, wsk)
    g = np.reshape(r, fut.shape)
    dec = temporal_decoder(g, fut, vp)
    return dec + (xq @ mxq(f64(wres), 0, "e4m3"))


def e4m3fn_bytes(y):
    return np.clip(np.asarray(y, np.float64), -448.0, 448.0).astype(np.float32).astype(ml_dtypes.float8_e4m3fn).view(np.uint8)


def e4m3fn_values(b):
    return np.asarray(b, np.uint8).view(ml_dtypes.float8_e4m3fn).astype(np.float64)


def setup_inputs():
    d = draw0()
    x0 = np.asarray(d['x']).astype(np.float64)
    s = (np.max(np.abs(x0), axis=(0,), keepdims=True) / 448.0).astype(np.float32)
    out = {}
    for k, v in d.items():
        if k == 'x':
            out['x_bytes'] = e4m3fn_bytes(x0 / s.astype(np.float64))
            out['x_scale'] = s
        else:
            out[k] = v
    return out


def reference(x_bytes, x_scale, fut, w1, w2, wsk, vp, wres):
    return core(e4m3fn_values(x_bytes) * x_scale.astype(np.float64), fut, w1, w2, wsk, vp, wres)

@@ -1,0 +1,346 @@
+from contextlib import ExitStack
+
+import concourse.mybir as mybir
+from concourse.masks import make_identity
+
+N, L, F, H, P_DEC = 4096, 512, 512, 256, 4
+PH = P_DEC * H
+FLOPS = 2 * N * (L * F + F * PH + L * PH + L * H)
+
+F32 = mybir.dt.float32
+BF16 = mybir.dt.bfloat16
+U32 = mybir.dt.uint32
+U8 = mybir.dt.uint8
+FP8 = mybir.dt.float8_e4m3fn
+FP8X4 = mybir.dt.float8_e4m3fn_x4
+ADD = mybir.AluOpType.add
+MULT = mybir.AluOpType.mult
+RELU = mybir.ActivationFunctionType.Relu
+
+P = 128
+STEP = 256
+STEPS = N // STEP
+GROUPS = [1, 1, 2, 4, 4, 4]
+SPLIT = 256
+ON_VECTOR = (0, 1)
+
+
+def tile_tideresidualencodertemporaldecoder_t_kernel(
+    tc, x_bytes, x_scale, fut, w1, w2, wsk, vp, wres, out
+):
+    nc = tc.nc
+    with ExitStack() as ctx:
+        keep = ctx.enter_context(tc.tile_pool(name="keep", bufs=1))
+        work = ctx.enter_context(tc.tile_pool(name="work", bufs=2))
+        psum = ctx.enter_context(tc.psum_pool(name="psum", bufs=1))
+        ctx.enter_context(tc.manual_schedule())
+
+        place = []
+        x_view, fut_view, out_view = [], [], []
+        row0 = 0
+        for count in GROUPS:
+            rows = slice(row0, row0 + count * STEP)
+            x_view.append(x_bytes[rows, :].rearrange("(p i) k -> p i k", p=P))
+            fut_view.append(fut[rows, :, :].rearrange("(p i) q j -> p i (q j)", p=P))
+            out_view.append(out[rows, :].rearrange("(p i) j -> p i j", p=P))
+            for j in range(count):
+                place.append((len(x_view) - 1, j))
+            row0 += count * STEP
+
+        x_in, fut_in = {}, {}
+
+        def load_x(g):
+            n = GROUPS[g]
+            t = keep.tile([P, 2 * n, L], U8, name=f"xbytes{g}", align_bytes=64)
+            nc.sync.dma_start(out=t[:], in_=x_view[g])
+            x_in[g] = t
+
+        def load_fut(s):
+            g, j = place[s]
+            t = keep.tile([P, 2, PH], BF16, name=f"fut{s}")
+            nc.sync.dma_start(out=t[:], in_=fut_view[g][:, 2 * j : 2 * j + 2, :])
+            fut_in[s] = t
+
+        def load_w(name, w, cols):
+            t = keep.tile([P, 4, cols.stop - cols.start], BF16, name=name)
+            nc.sync.dma_start(out=t[:], in_=w.rearrange("(p j) c -> p j c", j=4)[:, :, cols])
+            return t
+
+        scale = keep.tile([P, L], F32, name="scale")
+        nc.scalar.dma_start(out=scale[:], in_=x_scale.rearrange("o k -> (o k)").partition_broadcast(P))
+        load_x(0)
+        w1_raw = load_w("w1_raw", w1, slice(0, F))
+        load_x(1)
+        wsk_raw = [load_w(f"wsk_raw{b}", wsk, slice(512 * b, 512 * b + 512)) for b in range(2)]
+        w2_raw = [load_w(f"w2_raw{b}", w2, slice(512 * b, 512 * b + 512)) for b in range(2)]
+        wres_raw = load_w("wres_raw", wres, slice(0, H))
+        vp_bf = keep.tile([P, P_DEC], BF16, name="vp_bf")
+        nc.sync.dma_start(out=vp_bf[:], in_=vp.partition_broadcast(P))
+        load_fut(0)
+        load_x(2)
+        load_fut(1)
+        load_fut(2)
+        load_x(3)
+        for s in range(3, 8):
+            load_fut(s)
+        load_x(4)
+        for s in range(8, 12):
+            load_fut(s)
+        load_x(5)
+        for s in range(12, 16):
+            load_fut(s)
+
+        warm = keep.tile([P, 1], F32, name="warm")
+        nc.vector.memset(warm[:], 0.0)
+        nc.scalar.activation(out=warm[:], in_=warm[:], func=RELU)
+        ident = keep.tile([P, P], F32, name="ident")
+        make_identity(nc, ident[:])
+
+        xc, xb, xg, xq, xs, hg, hq, hs, xt, hb, rb, res, zt, acc = ({} for i in range(14))
+
+        def x_bytes_of(s):
+            g, j = place[s]
+            return x_in[g][:, 2 * j : 2 * j + 2, :].rearrange("p i k -> p (i k)").bitcast(FP8)
+
+        def widen_vector(s, i):
+            if i == 0:
+                xb[s] = work.tile([P, 2 * L], BF16, name="xb", bufs=3, align_bytes=64)
+            cols = slice(i * L, i * L + L)
+            nc.vector.tensor_tensor(out=xb[s][:, cols], in0=x_bytes_of(s)[:, cols], in1=scale[:], op=MULT)
+
+        def cast(s):
+            xc[s] = work.tile([P, 2 * L], BF16, name="xc")
+            nc.scalar.copy(out=xc[s][:], in_=x_bytes_of(s))
+
+        def widen_gpsimd(s):
+            xb[s] = work.tile([P, 2 * L], BF16, name="xb", bufs=3, align_bytes=64)
+            for i in range(2):
+                cols = slice(i * L, i * L + L)
+                nc.gpsimd.tensor_tensor(out=xb[s][:, cols], in0=xc[s][:, cols], in1=scale[:], op=MULT)
+
+        def transposes(s):
+            xt[s] = psum.tile([P, 512], F32, name="xt", bufs=1)
+            words = xb[s][:].bitcast(F32)
+            for i in range(2):
+                for u in range(2):
+                    nc.tensor.transpose(
+                        xt[s][:, (2 * i + u) * P : (2 * i + u + 1) * P],
+                        words[:, 256 * i + u : 256 * (i + 1) : 2],
+                        ident[:],
+                    )
+
+        def empty_x(s):
+            xg[s] = work.tile([P, 4 * STEP], BF16, name="xg", align_bytes=64)
+            nc.scalar.copy(
+                out=xg[s][:].bitcast(F32).rearrange("q (i p u) -> q i p u", i=2, u=2),
+                in_=xt[s][:].rearrange("q (i u p) -> q i p u", i=2, u=2),
+            )
+
+        def quantize_x(s):
+            xq[s] = work.tile([P, STEP], U32, name="xq", bufs=4, align_bytes=64)
+            xs[s] = work.tile([P, STEP], U8, name="xs", bufs=4, align_bytes=64)
+            nc.vector.quantize_mx(out=xq[s][:].bitcast(FP8X4), scales=xs[s][:], in_=xg[s][:])
+
+        def hidden(s):
+            for i in range(2):
+                hb[s, i] = psum.tile([P, 512], F32, name="hb", bufs=2)
+                cols = slice(i * P, i * P + P)
+                for t in range(4):
+                    part = slice(t * P, t * P + P)
+                    nc.tensor.matmul_mx(
+                        out=hb[s, i][:, part],
+                        lhsT=w1_q[:, part].bitcast(FP8X4), lhsT_scale=w1_s[:, part],
+                        rhs=xq[s][:, cols].bitcast(FP8X4), rhs_scale=xs[s][:, cols],
+                        start=True, stop=True,
+                    )
+
+        def relu_h(s):
+            hg[s] = work.tile([P, 4 * STEP], BF16, name="hg", align_bytes=64)
+            for i in range(2):
+                nc.scalar.activation(
+                    out=hg[s][:, 512 * i : 512 * i + 512].rearrange("m (n t) -> m n t", t=4),
+                    in_=hb[s, i][:].rearrange("m (t n) -> m n t", t=4),
+                    func=RELU,
+                )
+
+        def quantize_h(s):
+            hq[s] = work.tile([P, STEP], U32, name="hq", bufs=3, align_bytes=64)
+            hs[s] = work.tile([P, STEP], U8, name="hs", bufs=3, align_bytes=64)
+            nc.vector.quantize_mx(out=hq[s][:].bitcast(FP8X4), scales=hs[s][:], in_=hg[s][:])
+
+        def main(s):
+            for i in range(2):
+                cols = slice(i * P, i * P + P)
+                for b in range(2):
+                    rb[s, i, b] = psum.tile([P, 512], F32, name="rb", bufs=4)
+                    nc.tensor.matmul_mx(
+                        out=rb[s, i, b][:],
+                        lhsT=xq[s][:, cols].bitcast(FP8X4), lhsT_scale=xs[s][:, cols],
+                        rhs=wsk_q[b][:].bitcast(FP8X4), rhs_scale=wsk_s[b][:],
+                        start=True, stop=False,
+                    )
+                for b in range(2):
+                    nc.tensor.matmul_mx(
+                        out=rb[s, i, b][:],
+                        lhsT=hq[s][:, cols].bitcast(FP8X4), lhsT_scale=hs[s][:, cols],
+                        rhs=w2_q[b][:].bitcast(FP8X4), rhs_scale=w2_s[b][:],
+                        start=False, stop=True,
+                    )
+
+        def skip(s):
+            res[s] = psum.tile([P, 512], F32, name="res", bufs=1)
+            for i in range(2):
+                cols = slice(i * P, i * P + P)
+                nc.tensor.matmul_mx(
+                    out=res[s][:, H * i : H * i + H],
+                    lhsT=xq[s][:, cols].bitcast(FP8X4), lhsT_scale=xs[s][:, cols],
+                    rhs=wres_q[:].bitcast(FP8X4), rhs_scale=wres_s[:],
+                    start=True, stop=True,
+                )
+
+        def add_fut(s):
+            zt[s] = work.tile([P, 2, PH], F32, name="zt", bufs=3)
+            for i in range(2):
+                for b in range(2):
+                    cols = slice(512 * b, 512 * b + 512)
+                    nc.vector.tensor_tensor(
+                        out=zt[s][:, i, cols], in0=rb[s, i, b][:], in1=fut_in[s][:, i, cols], op=ADD
+                    )
+
+        def relu_z(s):
+            width = PH if s < STEPS - 1 else 512
+            for i in range(2):
+                for c in range(0, PH, width):
+                    cols = slice(c, c + width)
+                    nc.scalar.activation(out=zt[s][:, i, cols], in_=zt[s][:, i, cols], func=RELU)
+
+        def weigh(s, p, i=None):
+            sel = slice(0, 2) if i is None else slice(i, i + 1)
+            if p == 0:
+                if s not in acc:
+                    acc[s] = work.tile([P, 2, H], F32, name="acc", bufs=3)
+                add = res[s][:].rearrange("p (i j) -> p i j", i=2)[:, sel, :]
+            else:
+                add = acc[s][:, sel, :]
+            nc.vector.scalar_tensor_tensor(
+                out=acc[s][:, sel, :], in0=zt[s][:, sel, H * p : H * p + H],
+                scalar=vp_f[:, p : p + 1], in1=add, op0=MULT, op1=ADD,
+            )
+
+        def store(s, i=None):
+            g, j = place[s]
+            sel = slice(0, 2) if i is None else slice(i, i + 1)
+            nc.sync.dma_start(
+                out=out_view[g][:, 2 * j + sel.start : 2 * j + sel.stop, :], in_=acc[s][:, sel, :]
+            )
+
+        def quantize_w(name, group):
+            width = group.shape[1] // 4
+            q = keep.tile([P, width], U32, name=name + "_q", align_bytes=64)
+            sc = keep.tile([P, width], U8, name=name + "_s", align_bytes=64)
+            nc.vector.quantize_mx(out=q[:].bitcast(FP8X4), scales=sc[:], in_=group[:])
+            return q, sc
+
+        def interleave(name, raw, split):
+            width = raw.shape[2]
+            group = keep.tile([P, 4 * width], BF16, name=name + "_g", align_bytes=64)
+            view = group[:].rearrange("p (c i j) -> p c j i", i=4, j=4)
+            src = raw[:].rearrange("p j (c i) -> p c j i", i=4)
+            c = split // 4
+            nc.vector.tensor_copy(out=view[:, :c], in_=src[:, :c])
+            if split < width:
+                nc.scalar.copy(out=view[:, c:], in_=src[:, c:])
+            return group
+
+        widen_vector(0, 0)
+        widen_vector(0, 1)
+        transposes(0)
+        empty_x(0)
+        w1_g = keep.tile([P, 4 * F], BF16, name="w1_g", align_bytes=64)
+        dst = w1_g[:].rearrange("p (t m j) -> p t m j", t=4, j=4)
+        src = w1_raw[:].rearrange("p j (m t) -> p t m j", t=4)
+        nc.vector.tensor_copy(out=dst[:, 0:2], in_=src[:, 0:2])
+        nc.scalar.copy(out=dst[:, 2:4], in_=src[:, 2:4])
+        quantize_x(0)
+        w1_q, w1_s = quantize_w("w1", w1_g)
+        hidden(0)
+        widen_vector(1, 0)
+        widen_vector(1, 1)
+        transposes(1)
+        relu_h(0)
+        wsk_q, wsk_s, w2_q, w2_s = [None] * 2, [None] * 2, [None] * 2, [None] * 2
+        g0 = interleave("wsk0", wsk_raw[0], SPLIT)
+        empty_x(1)
+        quantize_h(0)
+        wsk_q[0], wsk_s[0] = quantize_w("wsk0", g0)
+        g1 = interleave("wsk1", wsk_raw[1], SPLIT)
+        quantize_x(1)
+        wsk_q[1], wsk_s[1] = quantize_w("wsk1", g1)
+        g2 = interleave("w20", w2_raw[0], SPLIT)
+        if 2 not in ON_VECTOR:
+            cast(2)
+            widen_gpsimd(2)
+            cast(3)
+            widen_gpsimd(3)
+        w2_q[0], w2_s[0] = quantize_w("w20", g2)
+        g3 = interleave("w21", w2_raw[1], SPLIT)
+        w2_q[1], w2_s[1] = quantize_w("w21", g3)
+        g4 = interleave("wres", wres_raw, H)
+        vp_f = keep.tile([P, P_DEC], F32, name="vp_f")
+        nc.vector.tensor_copy(out=vp_f[:], in_=vp_bf[:])
+        wres_q, wres_s = quantize_w("wres", g4)
+        if 2 in ON_VECTOR:
+            widen_vector(2, 0)
+            widen_vector(2, 1)
+            widen_vector(3, 0)
+            widen_vector(3, 1)
+
+        for s in range(STEPS + 1):
+            now, prev = s < STEPS, s >= 1
+            nxt, nx2, nx4 = s + 1 < STEPS, s + 2 < STEPS, s + 4 < STEPS
+            if now:
+                main(s)
+            if nxt:
+                hidden(s + 1)
+            if nx2:
+                transposes(s + 2)
+            if now:
+                skip(s)
+                add_fut(s)
+            if nxt:
+                relu_h(s + 1)
+            if nx2:
+                empty_x(s + 2)
+            if now:
+                relu_z(s)
+            if nx4 and s + 4 not in ON_VECTOR:
+                cast(s + 4)
+                widen_gpsimd(s + 4)
+            if prev and now:
+                weigh(s - 1, 0)
+            if nxt:
+                quantize_h(s + 1)
+            if nx2:
+                quantize_x(s + 2)
+            if prev and now:
+                weigh(s - 1, 1)
+            on_v = nx4 and s + 4 in ON_VECTOR
+            if prev and now:
+                if on_v:
+                    weigh(s - 1, 2)
+                    widen_vector(s + 4, 0)
+                    weigh(s - 1, 3)
+                    widen_vector(s + 4, 1)
+                else:
+                    for p in (2, 3):
+                        for i in range(2):
+                            weigh(s - 1, p, i)
+                store(s - 1)
+            elif on_v:
+                widen_vector(s + 4, 0)
+                widen_vector(s + 4, 1)
+            if not now:
+                for i in range(2):
+                    for p in range(4):
+                        weigh(s - 1, p, i)
+                    store(s - 1, i)

@@ -18,10 +18,12 @@ MULT = mybir.AluOpType.mult
 RELU = mybir.ActivationFunctionType.Relu
 
 P = 128
+GATE = True
 STEP = 256
 STEPS = N // STEP
 GROUPS = [1, 1, 2, 4, 4, 4]
-SPLIT = 256
+W1E = "VS"
+WE = "SSVSVSVSV"
 ON_VECTOR = (0, 1)
 
 
@@ -95,6 +97,8 @@ def tile_tideresidualencodertemporaldecoder_t_kernel(
         nc.scalar.activation(out=warm[:], in_=warm[:], func=RELU)
         ident = keep.tile([P, P], F32, name="ident")
         make_identity(nc, ident[:])
+        ident_bf = keep.tile([P, P], BF16, name="ident_bf")
+        make_identity(nc, ident_bf[:])
 
         xc, xb, xg, xq, xs, hg, hq, hs, xt, hb, rb, res, zt, acc = ({} for i in range(14))
 
@@ -112,8 +116,13 @@ def tile_tideresidualencodertemporaldecoder_t_kernel(
             xc[s] = work.tile([P, 2 * L], BF16, name="xc")
             nc.scalar.copy(out=xc[s][:], in_=x_bytes_of(s))
 
-        def widen_gpsimd(s):
+        def gate_gpsimd(s):
             xb[s] = work.tile([P, 2 * L], BF16, name="xb", bufs=3, align_bytes=64)
+            nc.vector.memset(xb[s][:, 0:2], 0.0)
+
+        def widen_gpsimd(s):
+            if s not in xb:
+                xb[s] = work.tile([P, 2 * L], BF16, name="xb", bufs=3, align_bytes=64)
             for i in range(2):
                 cols = slice(i * L, i * L + L)
                 nc.gpsimd.tensor_tensor(out=xb[s][:, cols], in0=xc[s][:, cols], in1=scale[:], op=MULT)
@@ -241,59 +250,67 @@ def tile_tideresidualencodertemporaldecoder_t_kernel(
             nc.vector.quantize_mx(out=q[:].bitcast(FP8X4), scales=sc[:], in_=group[:])
             return q, sc
 
-        def interleave(name, raw, split):
-            width = raw.shape[2]
-            group = keep.tile([P, 4 * width], BF16, name=name + "_g", align_bytes=64)
-            view = group[:].rearrange("p (c i j) -> p c j i", i=4, j=4)
-            src = raw[:].rearrange("p j (c i) -> p c j i", i=4)
-            c = split // 4
-            nc.vector.tensor_copy(out=view[:, :c], in_=src[:, :c])
-            if split < width:
-                nc.scalar.copy(out=view[:, c:], in_=src[:, c:])
-            return group
+        def spread(raw, group, c0, engine, view=None):
+            bank = psum.tile([P, 4, 256], BF16, name="wbank", tag="rb", bufs=4)
+            for j in range(4):
+                src = raw[:, j, c0 : c0 + 256] if view is None else view[:, j]
+                nc.tensor.matmul(out=bank[:, j, :], lhsT=ident_bf[:], rhs=src, start=True, stop=True)
+            dst = group[:, 4 * c0 : 4 * c0 + 1024].rearrange("p (c j) -> p c j", j=4)
+            src = bank[:].rearrange("p j c -> p c j")
+            if engine == "V":
+                nc.vector.tensor_copy(out=dst, in_=src)
+            else:
+                nc.scalar.copy(out=dst, in_=src)
+
+        def group_tile(name, width):
+            return keep.tile([P, 4 * width], BF16, name=name + "_g", align_bytes=64)
 
         widen_vector(0, 0)
         widen_vector(0, 1)
         transposes(0)
         empty_x(0)
-        w1_g = keep.tile([P, 4 * F], BF16, name="w1_g", align_bytes=64)
-        dst = w1_g[:].rearrange("p (t m j) -> p t m j", t=4, j=4)
-        src = w1_raw[:].rearrange("p j (m t) -> p t m j", t=4)
-        nc.vector.tensor_copy(out=dst[:, 0:2], in_=src[:, 0:2])
-        nc.scalar.copy(out=dst[:, 2:4], in_=src[:, 2:4])
+        w1_g = group_tile("w1", F)
+        w1_t = w1_raw[:].rearrange("p j (m t) -> p j t m", t=4)
+        for h in range(2):
+            spread(w1_raw, w1_g, 256 * h, W1E[h], w1_t[:, :, 2 * h : 2 * h + 2, :])
         quantize_x(0)
         w1_q, w1_s = quantize_w("w1", w1_g)
-        hidden(0)
+        wsk_q, wsk_s, w2_q, w2_s = [None] * 2, [None] * 2, [None] * 2, [None] * 2
+        wsk_g = [group_tile(f"wsk{b}", 512) for b in range(2)]
+        w2_g = [group_tile(f"w2{b}", 512) for b in range(2)]
+        wres_g = group_tile("wres", H)
+        spread(wsk_raw[0], wsk_g[0], 0, WE[0])
+        spread(wsk_raw[0], wsk_g[0], 256, WE[1])
         widen_vector(1, 0)
         widen_vector(1, 1)
+        hidden(0)
         transposes(1)
         relu_h(0)
-        wsk_q, wsk_s, w2_q, w2_s = [None] * 2, [None] * 2, [None] * 2, [None] * 2
-        g0 = interleave("wsk0", wsk_raw[0], SPLIT)
-        empty_x(1)
-        quantize_h(0)
-        wsk_q[0], wsk_s[0] = quantize_w("wsk0", g0)
-        g1 = interleave("wsk1", wsk_raw[1], SPLIT)
-        quantize_x(1)
-        wsk_q[1], wsk_s[1] = quantize_w("wsk1", g1)
-        g2 = interleave("w20", w2_raw[0], SPLIT)
-        if 2 not in ON_VECTOR:
-            cast(2)
-            widen_gpsimd(2)
-            cast(3)
-            widen_gpsimd(3)
-        w2_q[0], w2_s[0] = quantize_w("w20", g2)
-        g3 = interleave("w21", w2_raw[1], SPLIT)
-        w2_q[1], w2_s[1] = quantize_w("w21", g3)
-        g4 = interleave("wres", wres_raw, H)
-        vp_f = keep.tile([P, P_DEC], F32, name="vp_f")
-        nc.vector.tensor_copy(out=vp_f[:], in_=vp_bf[:])
-        wres_q, wres_s = quantize_w("wres", g4)
         if 2 in ON_VECTOR:
             widen_vector(2, 0)
             widen_vector(2, 1)
-            widen_vector(3, 0)
-            widen_vector(3, 1)
+        wsk_q[0], wsk_s[0] = quantize_w("wsk0", wsk_g[0])
+        spread(wsk_raw[1], wsk_g[1], 0, WE[2])
+        spread(wsk_raw[1], wsk_g[1], 256, WE[3])
+        empty_x(1)
+        quantize_h(0)
+        wsk_q[1], wsk_s[1] = quantize_w("wsk1", wsk_g[1])
+        spread(w2_raw[0], w2_g[0], 0, WE[4])
+        spread(w2_raw[0], w2_g[0], 256, WE[5])
+        quantize_x(1)
+        w2_q[0], w2_s[0] = quantize_w("w20", w2_g[0])
+        spread(w2_raw[1], w2_g[1], 0, WE[6])
+        spread(w2_raw[1], w2_g[1], 256, WE[7])
+        w2_q[1], w2_s[1] = quantize_w("w21", w2_g[1])
+        spread(wres_raw, wres_g, 0, WE[8])
+        if 2 not in ON_VECTOR:
+            cast(2)
+            widen_gpsimd(2)
+        vp_f = keep.tile([P, P_DEC], F32, name="vp_f")
+        nc.vector.tensor_copy(out=vp_f[:], in_=vp_bf[:])
+        wres_q, wres_s = quantize_w("wres", wres_g)
+        cast(3)
+        widen_gpsimd(3)
 
         for s in range(STEPS + 1):
             now, prev = s < STEPS, s >= 1
@@ -306,6 +323,9 @@ def tile_tideresidualencodertemporaldecoder_t_kernel(
                 transposes(s + 2)
             if now:
                 skip(s)
+            if nx4 and s + 4 not in ON_VECTOR and GATE:
+                gate_gpsimd(s + 4)
+            if now:
                 add_fut(s)
             if nxt:
                 relu_h(s + 1)

@@ -18,13 +18,12 @@ MULT = mybir.AluOpType.mult
 RELU = mybir.ActivationFunctionType.Relu
 
 P = 128
-GATE = True
 STEP = 256
 STEPS = N // STEP
-GROUPS = [1, 1, 2, 4, 4, 4]
+GROUPS = [2, 2, 4, 4, 4]
 W1E = "VS"
 WE = "SSVSVSVSV"
-ON_VECTOR = (0, 1)
+ON_VECTOR = (0, 1, 2)
 
 
 def tile_tideresidualencodertemporaldecoder_t_kernel(
@@ -35,7 +34,6 @@ def tile_tideresidualencodertemporaldecoder_t_kernel(
         keep = ctx.enter_context(tc.tile_pool(name="keep", bufs=1))
         work = ctx.enter_context(tc.tile_pool(name="work", bufs=2))
         psum = ctx.enter_context(tc.psum_pool(name="psum", bufs=1))
-        ctx.enter_context(tc.manual_schedule())
 
         place = []
         x_view, fut_view, out_view = [], [], []
@@ -51,11 +49,12 @@ def tile_tideresidualencodertemporaldecoder_t_kernel(
 
         x_in, fut_in = {}, {}
 
-        def load_x(g):
-            n = GROUPS[g]
-            t = keep.tile([P, 2 * n, L], U8, name=f"xbytes{g}", align_bytes=64)
-            nc.sync.dma_start(out=t[:], in_=x_view[g])
-            x_in[g] = t
+        def load_x(g, first=0, count=None):
+            n = GROUPS[g] if count is None else count
+            t = keep.tile([P, 2 * n, L], U8, name=f"xbytes{g}_{first}", align_bytes=64)
+            nc.sync.dma_start(out=t[:], in_=x_view[g][:, 2 * first : 2 * (first + n), :])
+            for j in range(n):
+                x_in[g, first + j] = t[:, 2 * j : 2 * j + 2, :]
 
         def load_fut(s):
             g, j = place[s]
@@ -70,26 +69,25 @@ def tile_tideresidualencodertemporaldecoder_t_kernel(
 
         scale = keep.tile([P, L], F32, name="scale")
         nc.scalar.dma_start(out=scale[:], in_=x_scale.rearrange("o k -> (o k)").partition_broadcast(P))
-        load_x(0)
+        load_x(0, 0, 1)
         w1_raw = load_w("w1_raw", w1, slice(0, F))
-        load_x(1)
+        load_x(0, 1, 1)
         wsk_raw = [load_w(f"wsk_raw{b}", wsk, slice(512 * b, 512 * b + 512)) for b in range(2)]
         w2_raw = [load_w(f"w2_raw{b}", w2, slice(512 * b, 512 * b + 512)) for b in range(2)]
         wres_raw = load_w("wres_raw", wres, slice(0, H))
         vp_bf = keep.tile([P, P_DEC], BF16, name="vp_bf")
         nc.sync.dma_start(out=vp_bf[:], in_=vp.partition_broadcast(P))
+        load_x(1)
         load_fut(0)
-        load_x(2)
         load_fut(1)
-        load_fut(2)
+        load_x(2)
+        for s in range(2, 6):
+            load_fut(s)
         load_x(3)
-        for s in range(3, 8):
+        for s in range(6, 10):
             load_fut(s)
         load_x(4)
-        for s in range(8, 12):
-            load_fut(s)
-        load_x(5)
-        for s in range(12, 16):
+        for s in range(10, 16):
             load_fut(s)
 
         warm = keep.tile([P, 1], F32, name="warm")
@@ -104,7 +102,7 @@ def tile_tideresidualencodertemporaldecoder_t_kernel(
 
         def x_bytes_of(s):
             g, j = place[s]
-            return x_in[g][:, 2 * j : 2 * j + 2, :].rearrange("p i k -> p (i k)").bitcast(FP8)
+            return x_in[g, j].rearrange("p i k -> p (i k)").bitcast(FP8)
 
         def widen_vector(s, i):
             if i == 0:
@@ -116,13 +114,8 @@ def tile_tideresidualencodertemporaldecoder_t_kernel(
             xc[s] = work.tile([P, 2 * L], BF16, name="xc")
             nc.scalar.copy(out=xc[s][:], in_=x_bytes_of(s))
 
-        def gate_gpsimd(s):
-            xb[s] = work.tile([P, 2 * L], BF16, name="xb", bufs=3, align_bytes=64)
-            nc.vector.memset(xb[s][:, 0:2], 0.0)
-
         def widen_gpsimd(s):
-            if s not in xb:
-                xb[s] = work.tile([P, 2 * L], BF16, name="xb", bufs=3, align_bytes=64)
+            xb[s] = work.tile([P, 2 * L], BF16, name="xb", bufs=3, align_bytes=64)
             for i in range(2):
                 cols = slice(i * L, i * L + L)
                 nc.gpsimd.tensor_tensor(out=xb[s][:, cols], in0=xc[s][:, cols], in1=scale[:], op=MULT)
@@ -146,8 +139,8 @@ def tile_tideresidualencodertemporaldecoder_t_kernel(
             )
 
         def quantize_x(s):
-            xq[s] = work.tile([P, STEP], U32, name="xq", bufs=4, align_bytes=64)
-            xs[s] = work.tile([P, STEP], U8, name="xs", bufs=4, align_bytes=64)
+            xq[s] = work.tile([P, STEP], U32, name="xq", bufs=5, align_bytes=64)
+            xs[s] = work.tile([P, STEP], U8, name="xs", bufs=5, align_bytes=64)
             nc.vector.quantize_mx(out=xq[s][:].bitcast(FP8X4), scales=xs[s][:], in_=xg[s][:])
 
         def hidden(s):
@@ -173,28 +166,27 @@ def tile_tideresidualencodertemporaldecoder_t_kernel(
                 )
 
         def quantize_h(s):
-            hq[s] = work.tile([P, STEP], U32, name="hq", bufs=3, align_bytes=64)
-            hs[s] = work.tile([P, STEP], U8, name="hs", bufs=3, align_bytes=64)
+            hq[s] = work.tile([P, STEP], U32, name="hq", bufs=4, align_bytes=64)
+            hs[s] = work.tile([P, STEP], U8, name="hs", bufs=4, align_bytes=64)
             nc.vector.quantize_mx(out=hq[s][:].bitcast(FP8X4), scales=hs[s][:], in_=hg[s][:])
 
-        def main(s):
-            for i in range(2):
-                cols = slice(i * P, i * P + P)
-                for b in range(2):
-                    rb[s, i, b] = psum.tile([P, 512], F32, name="rb", bufs=4)
-                    nc.tensor.matmul_mx(
-                        out=rb[s, i, b][:],
-                        lhsT=xq[s][:, cols].bitcast(FP8X4), lhsT_scale=xs[s][:, cols],
-                        rhs=wsk_q[b][:].bitcast(FP8X4), rhs_scale=wsk_s[b][:],
-                        start=True, stop=False,
-                    )
-                for b in range(2):
-                    nc.tensor.matmul_mx(
-                        out=rb[s, i, b][:],
-                        lhsT=hq[s][:, cols].bitcast(FP8X4), lhsT_scale=hs[s][:, cols],
-                        rhs=w2_q[b][:].bitcast(FP8X4), rhs_scale=w2_s[b][:],
-                        start=False, stop=True,
-                    )
+        def main(s, i):
+            cols = slice(i * P, i * P + P)
+            for b in range(2):
+                rb[s, i, b] = psum.tile([P, 512], F32, name="rb", bufs=4)
+                nc.tensor.matmul_mx(
+                    out=rb[s, i, b][:],
+                    lhsT=xq[s][:, cols].bitcast(FP8X4), lhsT_scale=xs[s][:, cols],
+                    rhs=wsk_q[b][:].bitcast(FP8X4), rhs_scale=wsk_s[b][:],
+                    start=True, stop=False,
+                )
+            for b in range(2):
+                nc.tensor.matmul_mx(
+                    out=rb[s, i, b][:],
+                    lhsT=hq[s][:, cols].bitcast(FP8X4), lhsT_scale=hs[s][:, cols],
+                    rhs=w2_q[b][:].bitcast(FP8X4), rhs_scale=w2_s[b][:],
+                    start=False, stop=True,
+                )
 
         def skip(s):
             res[s] = psum.tile([P, 512], F32, name="res", bufs=1)
@@ -207,40 +199,44 @@ def tile_tideresidualencodertemporaldecoder_t_kernel(
                     start=True, stop=True,
                 )
 
-        def add_fut(s):
-            zt[s] = work.tile([P, 2, PH], F32, name="zt", bufs=3)
-            for i in range(2):
-                for b in range(2):
-                    cols = slice(512 * b, 512 * b + 512)
-                    nc.vector.tensor_tensor(
-                        out=zt[s][:, i, cols], in0=rb[s, i, b][:], in1=fut_in[s][:, i, cols], op=ADD
-                    )
+        def add_fut(s, i):
+            q, half = s // 2, 2 * (s % 2)
+            if q not in zt:
+                zt[q] = work.tile([P, 4, PH], F32, name="zt", bufs=2)
+            for b in range(2):
+                cols = slice(512 * b, 512 * b + 512)
+                nc.vector.tensor_tensor(
+                    out=zt[q][:, half + i, cols], in0=rb[s, i, b][:], in1=fut_in[s][:, i, cols], op=ADD
+                )
 
-        def relu_z(s):
-            width = PH if s < STEPS - 1 else 512
-            for i in range(2):
-                for c in range(0, PH, width):
-                    cols = slice(c, c + width)
-                    nc.scalar.activation(out=zt[s][:, i, cols], in_=zt[s][:, i, cols], func=RELU)
+        def relu_z(s, pieces=1):
+            q, half = s // 2, 2 * (s % 2)
+            z = zt[q][:, half : half + 2, :].rearrange("p i c -> p (i c)")
+            width = 2 * PH // pieces
+            for c in range(pieces):
+                cols = slice(width * c, width * c + width)
+                nc.scalar.activation(out=z[:, cols], in_=z[:, cols], func=RELU)
 
-        def weigh(s, p, i=None):
-            sel = slice(0, 2) if i is None else slice(i, i + 1)
-            if p == 0:
-                if s not in acc:
-                    acc[s] = work.tile([P, 2, H], F32, name="acc", bufs=3)
-                add = res[s][:].rearrange("p (i j) -> p i j", i=2)[:, sel, :]
-            else:
-                add = acc[s][:, sel, :]
+        def weigh_first(s, rows=slice(0, 2)):
+            q, half = s // 2, 2 * (s % 2)
+            if q not in acc:
+                acc[q] = work.tile([P, 4, H], F32, name="acc", bufs=2)
+            to = slice(half + rows.start, half + rows.stop)
             nc.vector.scalar_tensor_tensor(
-                out=acc[s][:, sel, :], in0=zt[s][:, sel, H * p : H * p + H],
-                scalar=vp_f[:, p : p + 1], in1=add, op0=MULT, op1=ADD,
+                out=acc[q][:, to, :], in0=zt[q][:, to, 0:H], scalar=vp_f[:, 0:1],
+                in1=res[s][:].rearrange("p (i j) -> p i j", i=2)[:, rows, :], op0=MULT, op1=ADD,
             )
 
-        def store(s, i=None):
-            g, j = place[s]
-            sel = slice(0, 2) if i is None else slice(i, i + 1)
+        def weigh(q, p, rows=slice(0, 4)):
+            nc.vector.scalar_tensor_tensor(
+                out=acc[q][:, rows, :], in0=zt[q][:, rows, H * p : H * p + H],
+                scalar=vp_f[:, p : p + 1], in1=acc[q][:, rows, :], op0=MULT, op1=ADD,
+            )
+
+        def store(q, rows=slice(0, 4)):
+            g, j = place[2 * q]
             nc.sync.dma_start(
-                out=out_view[g][:, 2 * j + sel.start : 2 * j + sel.stop, :], in_=acc[s][:, sel, :]
+                out=out_view[g][:, 2 * j + rows.start : 2 * j + rows.stop, :], in_=acc[q][:, rows, :]
             )
 
         def quantize_w(name, group):
@@ -275,92 +271,92 @@ def tile_tideresidualencodertemporaldecoder_t_kernel(
             spread(w1_raw, w1_g, 256 * h, W1E[h], w1_t[:, :, 2 * h : 2 * h + 2, :])
         quantize_x(0)
         w1_q, w1_s = quantize_w("w1", w1_g)
+        widen_vector(1, 0)
+        widen_vector(1, 1)
+        hidden(0)
+        transposes(1)
+        relu_h(0)
+        empty_x(1)
         wsk_q, wsk_s, w2_q, w2_s = [None] * 2, [None] * 2, [None] * 2, [None] * 2
         wsk_g = [group_tile(f"wsk{b}", 512) for b in range(2)]
         w2_g = [group_tile(f"w2{b}", 512) for b in range(2)]
         wres_g = group_tile("wres", H)
         spread(wsk_raw[0], wsk_g[0], 0, WE[0])
         spread(wsk_raw[0], wsk_g[0], 256, WE[1])
-        widen_vector(1, 0)
-        widen_vector(1, 1)
-        hidden(0)
-        transposes(1)
-        relu_h(0)
+        quantize_h(0)
+        quantize_x(1)
+        wsk_q[0], wsk_s[0] = quantize_w("wsk0", wsk_g[0])
+        hidden(1)
+        relu_h(1)
+        spread(wsk_raw[1], wsk_g[1], 0, WE[2])
+        spread(wsk_raw[1], wsk_g[1], 256, WE[3])
         if 2 in ON_VECTOR:
             widen_vector(2, 0)
             widen_vector(2, 1)
-        wsk_q[0], wsk_s[0] = quantize_w("wsk0", wsk_g[0])
-        spread(wsk_raw[1], wsk_g[1], 0, WE[2])
-        spread(wsk_raw[1], wsk_g[1], 256, WE[3])
-        empty_x(1)
-        quantize_h(0)
+        else:
+            cast(2)
+            widen_gpsimd(2)
+        quantize_h(1)
         wsk_q[1], wsk_s[1] = quantize_w("wsk1", wsk_g[1])
         spread(w2_raw[0], w2_g[0], 0, WE[4])
         spread(w2_raw[0], w2_g[0], 256, WE[5])
-        quantize_x(1)
+        transposes(2)
         w2_q[0], w2_s[0] = quantize_w("w20", w2_g[0])
         spread(w2_raw[1], w2_g[1], 0, WE[6])
         spread(w2_raw[1], w2_g[1], 256, WE[7])
+        empty_x(2)
         w2_q[1], w2_s[1] = quantize_w("w21", w2_g[1])
         spread(wres_raw, wres_g, 0, WE[8])
-        if 2 not in ON_VECTOR:
-            cast(2)
-            widen_gpsimd(2)
+        quantize_x(2)
+        cast(3)
+        widen_gpsimd(3)
         vp_f = keep.tile([P, P_DEC], F32, name="vp_f")
         nc.vector.tensor_copy(out=vp_f[:], in_=vp_bf[:])
         wres_q, wres_s = quantize_w("wres", wres_g)
-        cast(3)
-        widen_gpsimd(3)
+        cast(4)
+        widen_gpsimd(4)
 
-        for s in range(STEPS + 1):
-            now, prev = s < STEPS, s >= 1
-            nxt, nx2, nx4 = s + 1 < STEPS, s + 2 < STEPS, s + 4 < STEPS
-            if now:
-                main(s)
-            if nxt:
-                hidden(s + 1)
-            if nx2:
-                transposes(s + 2)
-            if now:
-                skip(s)
-            if nx4 and s + 4 not in ON_VECTOR and GATE:
-                gate_gpsimd(s + 4)
-            if now:
-                add_fut(s)
-            if nxt:
-                relu_h(s + 1)
-            if nx2:
-                empty_x(s + 2)
-            if now:
-                relu_z(s)
-            if nx4 and s + 4 not in ON_VECTOR:
-                cast(s + 4)
-                widen_gpsimd(s + 4)
-            if prev and now:
-                weigh(s - 1, 0)
-            if nxt:
-                quantize_h(s + 1)
-            if nx2:
-                quantize_x(s + 2)
-            if prev and now:
-                weigh(s - 1, 1)
-            on_v = nx4 and s + 4 in ON_VECTOR
-            if prev and now:
-                if on_v:
-                    weigh(s - 1, 2)
-                    widen_vector(s + 4, 0)
-                    weigh(s - 1, 3)
-                    widen_vector(s + 4, 1)
-                else:
-                    for p in (2, 3):
-                        for i in range(2):
-                            weigh(s - 1, p, i)
-                store(s - 1)
-            elif on_v:
-                widen_vector(s + 4, 0)
-                widen_vector(s + 4, 1)
-            if not now:
-                for i in range(2):
-                    for p in range(4):
-                        weigh(s - 1, p, i)
-                    store(s - 1, i)
+        ctx.enter_context(tc.manual_schedule())
+        for s in range(STEPS):
+            q, odd = s // 2, s % 2
+            main(s, 0)
+            if s >= 1:
+                skip(s - 1)
+            main(s, 1)
+            if s + 2 < STEPS:
+                hidden(s + 2)
+            if s + 3 < STEPS:
+                transposes(s + 3)
+            add_fut(s, 0)
+            if odd and q >= 1:
+                weigh(q - 1, 2)
+            add_fut(s, 1)
+            if s + 2 < STEPS:
+                relu_h(s + 2)
+            if s + 3 < STEPS:
+                empty_x(s + 3)
+            relu_z(s, 4 if s == STEPS - 1 else 1)
+            if s + 5 < STEPS:
+                cast(s + 5)
+                widen_gpsimd(s + 5)
+            if s >= 1:
+                weigh_first(s - 1)
+            if s + 2 < STEPS:
+                quantize_h(s + 2)
+            if q >= 1:
+                weigh(q - 1, 3 if odd else 1)
+            if s + 3 < STEPS:
+                quantize_x(s + 3)
+            if odd and q >= 1:
+                store(q - 1)
+        last = STEPS // 2 - 1
+        skip(STEPS - 1)
+        for p in range(1, P_DEC):
+            weigh(last, p, slice(0, 2))
+        store(last, slice(0, 2))
+        for i in range(2):
+            weigh_first(STEPS - 1, slice(i, i + 1))
+        for p in range(1, P_DEC):
+            for i in range(2):
+                weigh(last, p, slice(2 + i, 3 + i))
+        store(last, slice(2, 4))

@@ -18,11 +18,13 @@ MULT = mybir.AluOpType.mult
 RELU = mybir.ActivationFunctionType.Relu
 
 P = 128
+SHARE = 384
+LEAD = 4
 STEP = 256
 STEPS = N // STEP
 GROUPS = [2, 2, 4, 4, 4]
 W1E = "VS"
-WE = "SSVSVSVSV"
+WE = "SSSSSSSSS"
 ON_VECTOR = (0, 1, 2)
 
 
@@ -67,8 +69,9 @@ def tile_tideresidualencodertemporaldecoder_t_kernel(
             nc.sync.dma_start(out=t[:], in_=w.rearrange("(p j) c -> p j c", j=4)[:, :, cols])
             return t
 
-        scale = keep.tile([P, L], F32, name="scale")
-        nc.scalar.dma_start(out=scale[:], in_=x_scale.rearrange("o k -> (o k)").partition_broadcast(P))
+        scale = keep.tile([P, 2 * L], F32, name="scale")
+        nc.scalar.dma_start(out=scale[:, 0:L], in_=x_scale.rearrange("o k -> (o k)").partition_broadcast(P))
+        nc.scalar.copy(out=scale[:, L : 2 * L], in_=scale[:, 0:L])
         load_x(0, 0, 1)
         w1_raw = load_w("w1_raw", w1, slice(0, F))
         load_x(0, 1, 1)
@@ -108,17 +111,18 @@ def tile_tideresidualencodertemporaldecoder_t_kernel(
             if i == 0:
                 xb[s] = work.tile([P, 2 * L], BF16, name="xb", bufs=3, align_bytes=64)
             cols = slice(i * L, i * L + L)
-            nc.vector.tensor_tensor(out=xb[s][:, cols], in0=x_bytes_of(s)[:, cols], in1=scale[:], op=MULT)
+            nc.vector.tensor_tensor(out=xb[s][:, cols], in0=x_bytes_of(s)[:, cols], in1=scale[:, 0:L], op=MULT)
 
         def cast(s):
             xc[s] = work.tile([P, 2 * L], BF16, name="xc")
-            nc.scalar.copy(out=xc[s][:], in_=x_bytes_of(s))
+            nc.scalar.copy(out=xc[s][:, SHARE:], in_=x_bytes_of(s)[:, SHARE:])
 
         def widen_gpsimd(s):
             xb[s] = work.tile([P, 2 * L], BF16, name="xb", bufs=3, align_bytes=64)
-            for i in range(2):
-                cols = slice(i * L, i * L + L)
-                nc.gpsimd.tensor_tensor(out=xb[s][:, cols], in0=xc[s][:, cols], in1=scale[:], op=MULT)
+            nc.vector.tensor_tensor(
+                out=xb[s][:, 0 : SHARE + 2], in0=x_bytes_of(s)[:, 0 : SHARE + 2], in1=scale[:, 0 : SHARE + 2], op=MULT
+            )
+            nc.gpsimd.tensor_tensor(out=xb[s][:, SHARE:], in0=xc[s][:, SHARE:], in1=scale[:, SHARE:], op=MULT)
 
         def transposes(s):
             xt[s] = psum.tile([P, 512], F32, name="xt", bufs=1)
@@ -313,8 +317,10 @@ def tile_tideresidualencodertemporaldecoder_t_kernel(
         vp_f = keep.tile([P, P_DEC], F32, name="vp_f")
         nc.vector.tensor_copy(out=vp_f[:], in_=vp_bf[:])
         wres_q, wres_s = quantize_w("wres", wres_g)
-        cast(4)
-        widen_gpsimd(4)
+        if LEAD == 5:
+            cast(4)
+            widen_gpsimd(4)
+        cast(LEAD)
 
         ctx.enter_context(tc.manual_schedule())
         for s in range(STEPS):
@@ -327,20 +333,21 @@ def tile_tideresidualencodertemporaldecoder_t_kernel(
                 hidden(s + 2)
             if s + 3 < STEPS:
                 transposes(s + 3)
+            if s + LEAD < STEPS:
+                widen_gpsimd(s + LEAD)
             add_fut(s, 0)
-            if odd and q >= 1:
-                weigh(q - 1, 2)
             add_fut(s, 1)
             if s + 2 < STEPS:
                 relu_h(s + 2)
             if s + 3 < STEPS:
                 empty_x(s + 3)
             relu_z(s, 4 if s == STEPS - 1 else 1)
-            if s + 5 < STEPS:
-                cast(s + 5)
-                widen_gpsimd(s + 5)
+            if s + LEAD + 1 < STEPS:
+                cast(s + LEAD + 1)
             if s >= 1:
                 weigh_first(s - 1)
+            if odd and q >= 1:
+                weigh(q - 1, 2)
             if s + 2 < STEPS:
                 quantize_h(s + 2)
             if q >= 1:

@@ -18,14 +18,13 @@ MULT = mybir.AluOpType.mult
 RELU = mybir.ActivationFunctionType.Relu
 
 P = 128
-SHARE = 384
+SHARE = 256
 LEAD = 4
 STEP = 256
 STEPS = N // STEP
 GROUPS = [2, 2, 4, 4, 4]
 W1E = "VS"
-WE = "SSSSSSSSS"
-ON_VECTOR = (0, 1, 2)
+WE = "SSSSSVSSS"
 
 
 def tile_tideresidualencodertemporaldecoder_t_kernel(
@@ -36,6 +35,7 @@ def tile_tideresidualencodertemporaldecoder_t_kernel(
         keep = ctx.enter_context(tc.tile_pool(name="keep", bufs=1))
         work = ctx.enter_context(tc.tile_pool(name="work", bufs=2))
         psum = ctx.enter_context(tc.psum_pool(name="psum", bufs=1))
+        ctx.enter_context(tc.manual_schedule())
 
         place = []
         x_view, fut_view, out_view = [], [], []
@@ -70,8 +70,8 @@ def tile_tideresidualencodertemporaldecoder_t_kernel(
             return t
 
         scale = keep.tile([P, 2 * L], F32, name="scale")
-        nc.scalar.dma_start(out=scale[:, 0:L], in_=x_scale.rearrange("o k -> (o k)").partition_broadcast(P))
-        nc.scalar.copy(out=scale[:, L : 2 * L], in_=scale[:, 0:L])
+        scale_col = keep.tile([P, 4], F32, name="scale_col")
+        nc.scalar.dma_start(out=scale_col[:], in_=x_scale.rearrange("o (n c) -> (o n) c", c=4))
         load_x(0, 0, 1)
         w1_raw = load_w("w1_raw", w1, slice(0, F))
         load_x(0, 1, 1)
@@ -79,7 +79,8 @@ def tile_tideresidualencodertemporaldecoder_t_kernel(
         w2_raw = [load_w(f"w2_raw{b}", w2, slice(512 * b, 512 * b + 512)) for b in range(2)]
         wres_raw = load_w("wres_raw", wres, slice(0, H))
         vp_bf = keep.tile([P, P_DEC], BF16, name="vp_bf")
-        nc.sync.dma_start(out=vp_bf[:], in_=vp.partition_broadcast(P))
+        nc.vector.memset(vp_bf[:], 0.0)
+        nc.sync.dma_start(out=vp_bf[0:1, :], in_=vp.rearrange("(o q) -> o q", o=1))
         load_x(1)
         load_fut(0)
         load_fut(1)
@@ -100,18 +101,20 @@ def tile_tideresidualencodertemporaldecoder_t_kernel(
         make_identity(nc, ident[:])
         ident_bf = keep.tile([P, P], BF16, name="ident_bf")
         make_identity(nc, ident_bf[:])
+        ones_bf = keep.tile([P, P], BF16, name="ones_bf")
+        nc.vector.memset(ones_bf[:], 1.0)
 
-        xc, xb, xg, xq, xs, hg, hq, hs, xt, hb, rb, res, zt, acc = ({} for i in range(14))
+        bank = psum.tile([P, 4, P], F32, name="sbank", tag="rb", bufs=4)
+        for c in range(4):
+            nc.tensor.transpose(bank[:, c, :], scale_col[:, c : c + 1].to_broadcast([P, P]), ident[:])
+        nc.scalar.copy(out=scale[:, 0:L].rearrange("p (n c) -> p n c", c=4), in_=bank[:].rearrange("p c n -> p n c"))
+        nc.scalar.copy(out=scale[:, L : 2 * L], in_=scale[:, 0:L])
+
+        xc, xb, xg, xq, xs, hg, hq, hs, xt, hb, rb, res, zt, acc, both = ({} for i in range(15))
 
         def x_bytes_of(s):
             g, j = place[s]
             return x_in[g, j].rearrange("p i k -> p (i k)").bitcast(FP8)
-
-        def widen_vector(s, i):
-            if i == 0:
-                xb[s] = work.tile([P, 2 * L], BF16, name="xb", bufs=3, align_bytes=64)
-            cols = slice(i * L, i * L + L)
-            nc.vector.tensor_tensor(out=xb[s][:, cols], in0=x_bytes_of(s)[:, cols], in1=scale[:, 0:L], op=MULT)
 
         def cast(s):
             xc[s] = work.tile([P, 2 * L], BF16, name="xc")
@@ -136,7 +139,10 @@ def tile_tideresidualencodertemporaldecoder_t_kernel(
                     )
 
         def empty_x(s):
-            xg[s] = work.tile([P, 4 * STEP], BF16, name="xg", align_bytes=64)
+            if s >= 3:
+                xg[s] = both[s - 1][:, 4 * STEP : 8 * STEP]
+            else:
+                xg[s] = work.tile([P, 4 * STEP], BF16, name="xg", align_bytes=64)
             nc.scalar.copy(
                 out=xg[s][:].bitcast(F32).rearrange("q (i p u) -> q i p u", i=2, u=2),
                 in_=xt[s][:].rearrange("q (i u p) -> q i p u", i=2, u=2),
@@ -161,13 +167,24 @@ def tile_tideresidualencodertemporaldecoder_t_kernel(
                     )
 
         def relu_h(s):
-            hg[s] = work.tile([P, 4 * STEP], BF16, name="hg", align_bytes=64)
+            if s >= 2 and s + 1 < STEPS:
+                both[s] = work.tile([P, 8 * STEP], BF16, name="both", align_bytes=64)
+                hg[s] = both[s][:, 0 : 4 * STEP]
+            else:
+                hg[s] = work.tile([P, 4 * STEP], BF16, name="hg", align_bytes=64)
             for i in range(2):
                 nc.scalar.activation(
                     out=hg[s][:, 512 * i : 512 * i + 512].rearrange("m (n t) -> m n t", t=4),
                     in_=hb[s, i][:].rearrange("m (t n) -> m n t", t=4),
                     func=RELU,
                 )
+
+        def quantize_both(s):
+            codes = work.tile([P, 2 * STEP], U32, name="codes", bufs=6, align_bytes=64)
+            scales = work.tile([P, 2 * STEP], U8, name="scales", bufs=6, align_bytes=64)
+            nc.vector.quantize_mx(out=codes[:].bitcast(FP8X4), scales=scales[:], in_=both[s][:])
+            hq[s], hs[s] = codes[:, 0:STEP], scales[:, 0:STEP]
+            xq[s + 1], xs[s + 1] = codes[:, STEP : 2 * STEP], scales[:, STEP : 2 * STEP]
 
         def quantize_h(s):
             hq[s] = work.tile([P, STEP], U32, name="hq", bufs=4, align_bytes=64)
@@ -265,64 +282,62 @@ def tile_tideresidualencodertemporaldecoder_t_kernel(
         def group_tile(name, width):
             return keep.tile([P, 4 * width], BF16, name=name + "_g", align_bytes=64)
 
-        widen_vector(0, 0)
-        widen_vector(0, 1)
-        transposes(0)
-        empty_x(0)
-        w1_g = group_tile("w1", F)
-        w1_t = w1_raw[:].rearrange("p j (m t) -> p j t m", t=4)
-        for h in range(2):
-            spread(w1_raw, w1_g, 256 * h, W1E[h], w1_t[:, :, 2 * h : 2 * h + 2, :])
-        quantize_x(0)
-        w1_q, w1_s = quantize_w("w1", w1_g)
-        widen_vector(1, 0)
-        widen_vector(1, 1)
-        hidden(0)
-        transposes(1)
-        relu_h(0)
-        empty_x(1)
         wsk_q, wsk_s, w2_q, w2_s = [None] * 2, [None] * 2, [None] * 2, [None] * 2
         wsk_g = [group_tile(f"wsk{b}", 512) for b in range(2)]
         w2_g = [group_tile(f"w2{b}", 512) for b in range(2)]
         wres_g = group_tile("wres", H)
+        w1_g = group_tile("w1", F)
+        w1_t = w1_raw[:].rearrange("p j (m t) -> p j t m", t=4)
+
+        def widen(s):
+            xb[s] = work.tile([P, 2 * L], BF16, name="xb", bufs=3, align_bytes=64)
+            parts = 2 if s == 0 else 1
+            for i in range(parts):
+                cols = slice(2 * L // parts * i, 2 * L // parts * (i + 1))
+                nc.vector.tensor_tensor(out=xb[s][:, cols], in0=x_bytes_of(s)[:, cols], in1=scale[:, 0 : cols.stop - cols.start], op=MULT)
+
+        widen(0)
+        transposes(0)
+        empty_x(0)
+        spread(w1_raw, w1_g, 0, W1E[0], w1_t[:, :, 0:2, :])
+        quantize_x(0)
+        spread(w1_raw, w1_g, 256, W1E[1], w1_t[:, :, 2:4, :])
+        w1_q, w1_s = quantize_w("w1", w1_g)
         spread(wsk_raw[0], wsk_g[0], 0, WE[0])
         spread(wsk_raw[0], wsk_g[0], 256, WE[1])
+        hidden(0)
+        relu_h(0)
+        widen(1)
+        wsk_q[0], wsk_s[0] = quantize_w("wsk0", wsk_g[0])
+        transposes(1)
+        empty_x(1)
         quantize_h(0)
         quantize_x(1)
-        wsk_q[0], wsk_s[0] = quantize_w("wsk0", wsk_g[0])
-        hidden(1)
-        relu_h(1)
+        vp_f = keep.tile([P, P_DEC], F32, name="vp_f")
+        vbank = psum.tile([P, P_DEC], F32, name="vbank", tag="rb", bufs=4)
+        nc.tensor.matmul(out=vbank[:], lhsT=ones_bf[:], rhs=vp_bf[:], start=True, stop=True)
+        nc.vector.tensor_copy(out=vp_f[:], in_=vbank[:])
         spread(wsk_raw[1], wsk_g[1], 0, WE[2])
+        widen(2)
         spread(wsk_raw[1], wsk_g[1], 256, WE[3])
-        if 2 in ON_VECTOR:
-            widen_vector(2, 0)
-            widen_vector(2, 1)
-        else:
-            cast(2)
-            widen_gpsimd(2)
-        quantize_h(1)
-        wsk_q[1], wsk_s[1] = quantize_w("wsk1", wsk_g[1])
+        widen(3)
         spread(w2_raw[0], w2_g[0], 0, WE[4])
         spread(w2_raw[0], w2_g[0], 256, WE[5])
-        transposes(2)
-        w2_q[0], w2_s[0] = quantize_w("w20", w2_g[0])
         spread(w2_raw[1], w2_g[1], 0, WE[6])
+        wsk_q[1], wsk_s[1] = quantize_w("wsk1", wsk_g[1])
+        w2_q[0], w2_s[0] = quantize_w("w20", w2_g[0])
+        hidden(1)
+        relu_h(1)
         spread(w2_raw[1], w2_g[1], 256, WE[7])
-        empty_x(2)
+        transposes(2)
         w2_q[1], w2_s[1] = quantize_w("w21", w2_g[1])
+        empty_x(2)
         spread(wres_raw, wres_g, 0, WE[8])
         quantize_x(2)
-        cast(3)
-        widen_gpsimd(3)
-        vp_f = keep.tile([P, P_DEC], F32, name="vp_f")
-        nc.vector.tensor_copy(out=vp_f[:], in_=vp_bf[:])
+        quantize_h(1)
         wres_q, wres_s = quantize_w("wres", wres_g)
-        if LEAD == 5:
-            cast(4)
-            widen_gpsimd(4)
         cast(LEAD)
 
-        ctx.enter_context(tc.manual_schedule())
         for s in range(STEPS):
             q, odd = s // 2, s % 2
             main(s, 0)
@@ -341,19 +356,19 @@ def tile_tideresidualencodertemporaldecoder_t_kernel(
                 relu_h(s + 2)
             if s + 3 < STEPS:
                 empty_x(s + 3)
-            relu_z(s, 4 if s == STEPS - 1 else 1)
             if s + LEAD + 1 < STEPS:
                 cast(s + LEAD + 1)
+            relu_z(s, 4 if s == STEPS - 1 else 1)
             if s >= 1:
                 weigh_first(s - 1)
             if odd and q >= 1:
                 weigh(q - 1, 2)
-            if s + 2 < STEPS:
+            if s + 3 < STEPS:
+                quantize_both(s + 2)
+            elif s + 2 < STEPS:
                 quantize_h(s + 2)
             if q >= 1:
                 weigh(q - 1, 3 if odd else 1)
-            if s + 3 < STEPS:
-                quantize_x(s + 3)
             if odd and q >= 1:
                 store(q - 1)
         last = STEPS // 2 - 1
@@ -366,4 +381,5 @@ def tile_tideresidualencodertemporaldecoder_t_kernel(
         for p in range(1, P_DEC):
             for i in range(2):
                 weigh(last, p, slice(2 + i, 3 + i))
-        store(last, slice(2, 4))
+                if p == P_DEC - 1:
+                    store(last, slice(2 + i, 3 + i))

from contextlib import ExitStack

import concourse.mybir as mybir
from concourse.masks import make_identity

N, L, F, H, P_DEC = 4096, 512, 512, 256, 4
PH = P_DEC * H
FLOPS = 2 * N * (L * F + F * PH + L * PH + L * H)

F32 = mybir.dt.float32
BF16 = mybir.dt.bfloat16
U32 = mybir.dt.uint32
U8 = mybir.dt.uint8
FP8 = mybir.dt.float8_e4m3fn
FP8X4 = mybir.dt.float8_e4m3fn_x4
ADD = mybir.AluOpType.add
MULT = mybir.AluOpType.mult
RELU = mybir.ActivationFunctionType.Relu

P = 128
SHARE = 256
LEAD = 4
STEP = 256
STEPS = N // STEP
GROUPS = [2, 2, 4, 4, 4]
W1E = "VS"
WE = "SSSSSVSSS"


def tile_tideresidualencodertemporaldecoder_t_kernel(
    tc, x_bytes, x_scale, fut, w1, w2, wsk, vp, wres, out
):
    nc = tc.nc
    with ExitStack() as ctx:
        keep = ctx.enter_context(tc.tile_pool(name="keep", bufs=1))
        work = ctx.enter_context(tc.tile_pool(name="work", bufs=2))
        psum = ctx.enter_context(tc.psum_pool(name="psum", bufs=1))
        ctx.enter_context(tc.manual_schedule())

        place = []
        x_view, fut_view, out_view = [], [], []
        row0 = 0
        for count in GROUPS:
            rows = slice(row0, row0 + count * STEP)
            x_view.append(x_bytes[rows, :].rearrange("(p i) k -> p i k", p=P))
            fut_view.append(fut[rows, :, :].rearrange("(p i) q j -> p i (q j)", p=P))
            out_view.append(out[rows, :].rearrange("(p i) j -> p i j", p=P))
            for j in range(count):
                place.append((len(x_view) - 1, j))
            row0 += count * STEP

        x_in, fut_in = {}, {}

        def load_x(g, first=0, count=None):
            n = GROUPS[g] if count is None else count
            t = keep.tile([P, 2 * n, L], U8, name=f"xbytes{g}_{first}", align_bytes=64)
            nc.sync.dma_start(out=t[:], in_=x_view[g][:, 2 * first : 2 * (first + n), :])
            for j in range(n):
                x_in[g, first + j] = t[:, 2 * j : 2 * j + 2, :]

        def load_fut(s):
            g, j = place[s]
            t = keep.tile([P, 2, PH], BF16, name=f"fut{s}")
            nc.sync.dma_start(out=t[:], in_=fut_view[g][:, 2 * j : 2 * j + 2, :])
            fut_in[s] = t

        def load_w(name, w, cols):
            t = keep.tile([P, 4, cols.stop - cols.start], BF16, name=name)
            nc.sync.dma_start(out=t[:], in_=w.rearrange("(p j) c -> p j c", j=4)[:, :, cols])
            return t

        scale = keep.tile([P, 2 * L], F32, name="scale")
        scale_col = keep.tile([P, 4], F32, name="scale_col")
        nc.scalar.dma_start(out=scale_col[:], in_=x_scale.rearrange("o (n c) -> (o n) c", c=4))
        load_x(0, 0, 1)
        w1_raw = load_w("w1_raw", w1, slice(0, F))
        load_x(0, 1, 1)
        wsk_raw = [load_w(f"wsk_raw{b}", wsk, slice(512 * b, 512 * b + 512)) for b in range(2)]
        w2_raw = [load_w(f"w2_raw{b}", w2, slice(512 * b, 512 * b + 512)) for b in range(2)]
        wres_raw = load_w("wres_raw", wres, slice(0, H))
        vp_bf = keep.tile([P, P_DEC], BF16, name="vp_bf")
        nc.vector.memset(vp_bf[:], 0.0)
        nc.sync.dma_start(out=vp_bf[0:1, :], in_=vp.rearrange("(o q) -> o q", o=1))
        load_x(1)
        load_fut(0)
        load_fut(1)
        load_x(2)
        for s in range(2, 6):
            load_fut(s)
        load_x(3)
        for s in range(6, 10):
            load_fut(s)
        load_x(4)
        for s in range(10, 16):
            load_fut(s)

        warm = keep.tile([P, 1], F32, name="warm")
        nc.vector.memset(warm[:], 0.0)
        nc.scalar.activation(out=warm[:], in_=warm[:], func=RELU)
        ident = keep.tile([P, P], F32, name="ident")
        make_identity(nc, ident[:])
        ident_bf = keep.tile([P, P], BF16, name="ident_bf")
        make_identity(nc, ident_bf[:])
        ones_bf = keep.tile([P, P], BF16, name="ones_bf")
        nc.vector.memset(ones_bf[:], 1.0)

        bank = psum.tile([P, 4, P], F32, name="sbank", tag="rb", bufs=4)
        for c in range(4):
            nc.tensor.transpose(bank[:, c, :], scale_col[:, c : c + 1].to_broadcast([P, P]), ident[:])
        nc.scalar.copy(out=scale[:, 0:L].rearrange("p (n c) -> p n c", c=4), in_=bank[:].rearrange("p c n -> p n c"))
        nc.scalar.copy(out=scale[:, L : 2 * L], in_=scale[:, 0:L])

        xc, xb, xg, xq, xs, hg, hq, hs, xt, hb, rb, res, zt, acc, both = ({} for i in range(15))

        def x_bytes_of(s):
            g, j = place[s]
            return x_in[g, j].rearrange("p i k -> p (i k)").bitcast(FP8)

        def cast(s):
            xc[s] = work.tile([P, 2 * L], BF16, name="xc")
            nc.scalar.copy(out=xc[s][:, SHARE:], in_=x_bytes_of(s)[:, SHARE:])

        def widen_gpsimd(s):
            xb[s] = work.tile([P, 2 * L], BF16, name="xb", bufs=3, align_bytes=64)
            nc.vector.tensor_tensor(
                out=xb[s][:, 0 : SHARE + 2], in0=x_bytes_of(s)[:, 0 : SHARE + 2], in1=scale[:, 0 : SHARE + 2], op=MULT
            )
            nc.gpsimd.tensor_tensor(out=xb[s][:, SHARE:], in0=xc[s][:, SHARE:], in1=scale[:, SHARE:], op=MULT)

        def transposes(s):
            xt[s] = psum.tile([P, 512], F32, name="xt", bufs=1)
            words = xb[s][:].bitcast(F32)
            for i in range(2):
                for u in range(2):
                    nc.tensor.transpose(
                        xt[s][:, (2 * i + u) * P : (2 * i + u + 1) * P],
                        words[:, 256 * i + u : 256 * (i + 1) : 2],
                        ident[:],
                    )

        def empty_x(s):
            if s >= 3:
                xg[s] = both[s - 1][:, 4 * STEP : 8 * STEP]
            else:
                xg[s] = work.tile([P, 4 * STEP], BF16, name="xg", align_bytes=64)
            nc.scalar.copy(
                out=xg[s][:].bitcast(F32).rearrange("q (i p u) -> q i p u", i=2, u=2),
                in_=xt[s][:].rearrange("q (i u p) -> q i p u", i=2, u=2),
            )

        def quantize_x(s):
            xq[s] = work.tile([P, STEP], U32, name="xq", bufs=5, align_bytes=64)
            xs[s] = work.tile([P, STEP], U8, name="xs", bufs=5, align_bytes=64)
            nc.vector.quantize_mx(out=xq[s][:].bitcast(FP8X4), scales=xs[s][:], in_=xg[s][:])

        def hidden(s):
            for i in range(2):
                hb[s, i] = psum.tile([P, 512], F32, name="hb", bufs=2)
                cols = slice(i * P, i * P + P)
                for t in range(4):
                    part = slice(t * P, t * P + P)
                    nc.tensor.matmul_mx(
                        out=hb[s, i][:, part],
                        lhsT=w1_q[:, part].bitcast(FP8X4), lhsT_scale=w1_s[:, part],
                        rhs=xq[s][:, cols].bitcast(FP8X4), rhs_scale=xs[s][:, cols],
                        start=True, stop=True,
                    )

        def relu_h(s):
            if s >= 2 and s + 1 < STEPS:
                both[s] = work.tile([P, 8 * STEP], BF16, name="both", align_bytes=64)
                hg[s] = both[s][:, 0 : 4 * STEP]
            else:
                hg[s] = work.tile([P, 4 * STEP], BF16, name="hg", align_bytes=64)
            for i in range(2):
                nc.scalar.activation(
                    out=hg[s][:, 512 * i : 512 * i + 512].rearrange("m (n t) -> m n t", t=4),
                    in_=hb[s, i][:].rearrange("m (t n) -> m n t", t=4),
                    func=RELU,
                )

        def quantize_both(s):
            codes = work.tile([P, 2 * STEP], U32, name="codes", bufs=6, align_bytes=64)
            scales = work.tile([P, 2 * STEP], U8, name="scales", bufs=6, align_bytes=64)
            nc.vector.quantize_mx(out=codes[:].bitcast(FP8X4), scales=scales[:], in_=both[s][:])
            hq[s], hs[s] = codes[:, 0:STEP], scales[:, 0:STEP]
            xq[s + 1], xs[s + 1] = codes[:, STEP : 2 * STEP], scales[:, STEP : 2 * STEP]

        def quantize_h(s):
            hq[s] = work.tile([P, STEP], U32, name="hq", bufs=4, align_bytes=64)
            hs[s] = work.tile([P, STEP], U8, name="hs", bufs=4, align_bytes=64)
            nc.vector.quantize_mx(out=hq[s][:].bitcast(FP8X4), scales=hs[s][:], in_=hg[s][:])

        def main(s, i):
            cols = slice(i * P, i * P + P)
            for b in range(2):
                rb[s, i, b] = psum.tile([P, 512], F32, name="rb", bufs=4)
                nc.tensor.matmul_mx(
                    out=rb[s, i, b][:],
                    lhsT=xq[s][:, cols].bitcast(FP8X4), lhsT_scale=xs[s][:, cols],
                    rhs=wsk_q[b][:].bitcast(FP8X4), rhs_scale=wsk_s[b][:],
                    start=True, stop=False,
                )
            for b in range(2):
                nc.tensor.matmul_mx(
                    out=rb[s, i, b][:],
                    lhsT=hq[s][:, cols].bitcast(FP8X4), lhsT_scale=hs[s][:, cols],
                    rhs=w2_q[b][:].bitcast(FP8X4), rhs_scale=w2_s[b][:],
                    start=False, stop=True,
                )

        def skip(s):
            res[s] = psum.tile([P, 512], F32, name="res", bufs=1)
            for i in range(2):
                cols = slice(i * P, i * P + P)
                nc.tensor.matmul_mx(
                    out=res[s][:, H * i : H * i + H],
                    lhsT=xq[s][:, cols].bitcast(FP8X4), lhsT_scale=xs[s][:, cols],
                    rhs=wres_q[:].bitcast(FP8X4), rhs_scale=wres_s[:],
                    start=True, stop=True,
                )

        def add_fut(s, i):
            q, half = s // 2, 2 * (s % 2)
            if q not in zt:
                zt[q] = work.tile([P, 4, PH], F32, name="zt", bufs=2)
            for b in range(2):
                cols = slice(512 * b, 512 * b + 512)
                nc.vector.tensor_tensor(
                    out=zt[q][:, half + i, cols], in0=rb[s, i, b][:], in1=fut_in[s][:, i, cols], op=ADD
                )

        def relu_z(s, pieces=1):
            q, half = s // 2, 2 * (s % 2)
            z = zt[q][:, half : half + 2, :].rearrange("p i c -> p (i c)")
            width = 2 * PH // pieces
            for c in range(pieces):
                cols = slice(width * c, width * c + width)
                nc.scalar.activation(out=z[:, cols], in_=z[:, cols], func=RELU)

        def weigh_first(s, rows=slice(0, 2)):
            q, half = s // 2, 2 * (s % 2)
            if q not in acc:
                acc[q] = work.tile([P, 4, H], F32, name="acc", bufs=2)
            to = slice(half + rows.start, half + rows.stop)
            nc.vector.scalar_tensor_tensor(
                out=acc[q][:, to, :], in0=zt[q][:, to, 0:H], scalar=vp_f[:, 0:1],
                in1=res[s][:].rearrange("p (i j) -> p i j", i=2)[:, rows, :], op0=MULT, op1=ADD,
            )

        def weigh(q, p, rows=slice(0, 4)):
            nc.vector.scalar_tensor_tensor(
                out=acc[q][:, rows, :], in0=zt[q][:, rows, H * p : H * p + H],
                scalar=vp_f[:, p : p + 1], in1=acc[q][:, rows, :], op0=MULT, op1=ADD,
            )

        def store(q, rows=slice(0, 4)):
            g, j = place[2 * q]
            nc.sync.dma_start(
                out=out_view[g][:, 2 * j + rows.start : 2 * j + rows.stop, :], in_=acc[q][:, rows, :]
            )

        def quantize_w(name, group):
            width = group.shape[1] // 4
            q = keep.tile([P, width], U32, name=name + "_q", align_bytes=64)
            sc = keep.tile([P, width], U8, name=name + "_s", align_bytes=64)
            nc.vector.quantize_mx(out=q[:].bitcast(FP8X4), scales=sc[:], in_=group[:])
            return q, sc

        def spread(raw, group, c0, engine, view=None):
            bank = psum.tile([P, 4, 256], BF16, name="wbank", tag="rb", bufs=4)
            for j in range(4):
                src = raw[:, j, c0 : c0 + 256] if view is None else view[:, j]
                nc.tensor.matmul(out=bank[:, j, :], lhsT=ident_bf[:], rhs=src, start=True, stop=True)
            dst = group[:, 4 * c0 : 4 * c0 + 1024].rearrange("p (c j) -> p c j", j=4)
            src = bank[:].rearrange("p j c -> p c j")
            if engine == "V":
                nc.vector.tensor_copy(out=dst, in_=src)
            else:
                nc.scalar.copy(out=dst, in_=src)

        def group_tile(name, width):
            return keep.tile([P, 4 * width], BF16, name=name + "_g", align_bytes=64)

        wsk_q, wsk_s, w2_q, w2_s = [None] * 2, [None] * 2, [None] * 2, [None] * 2
        wsk_g = [group_tile(f"wsk{b}", 512) for b in range(2)]
        w2_g = [group_tile(f"w2{b}", 512) for b in range(2)]
        wres_g = group_tile("wres", H)
        w1_g = group_tile("w1", F)
        w1_t = w1_raw[:].rearrange("p j (m t) -> p j t m", t=4)

        def widen(s):
            xb[s] = work.tile([P, 2 * L], BF16, name="xb", bufs=3, align_bytes=64)
            parts = 2 if s == 0 else 1
            for i in range(parts):
                cols = slice(2 * L // parts * i, 2 * L // parts * (i + 1))
                nc.vector.tensor_tensor(out=xb[s][:, cols], in0=x_bytes_of(s)[:, cols], in1=scale[:, 0 : cols.stop - cols.start], op=MULT)

        widen(0)
        transposes(0)
        empty_x(0)
        spread(w1_raw, w1_g, 0, W1E[0], w1_t[:, :, 0:2, :])
        quantize_x(0)
        spread(w1_raw, w1_g, 256, W1E[1], w1_t[:, :, 2:4, :])
        w1_q, w1_s = quantize_w("w1", w1_g)
        spread(wsk_raw[0], wsk_g[0], 0, WE[0])
        spread(wsk_raw[0], wsk_g[0], 256, WE[1])
        hidden(0)
        relu_h(0)
        widen(1)
        wsk_q[0], wsk_s[0] = quantize_w("wsk0", wsk_g[0])
        transposes(1)
        empty_x(1)
        quantize_h(0)
        quantize_x(1)
        vp_f = keep.tile([P, P_DEC], F32, name="vp_f")
        vbank = psum.tile([P, P_DEC], F32, name="vbank", tag="rb", bufs=4)
        nc.tensor.matmul(out=vbank[:], lhsT=ones_bf[:], rhs=vp_bf[:], start=True, stop=True)
        nc.vector.tensor_copy(out=vp_f[:], in_=vbank[:])
        spread(wsk_raw[1], wsk_g[1], 0, WE[2])
        widen(2)
        spread(wsk_raw[1], wsk_g[1], 256, WE[3])
        widen(3)
        spread(w2_raw[0], w2_g[0], 0, WE[4])
        spread(w2_raw[0], w2_g[0], 256, WE[5])
        spread(w2_raw[1], w2_g[1], 0, WE[6])
        wsk_q[1], wsk_s[1] = quantize_w("wsk1", wsk_g[1])
        w2_q[0], w2_s[0] = quantize_w("w20", w2_g[0])
        hidden(1)
        relu_h(1)
        spread(w2_raw[1], w2_g[1], 256, WE[7])
        transposes(2)
        w2_q[1], w2_s[1] = quantize_w("w21", w2_g[1])
        empty_x(2)
        spread(wres_raw, wres_g, 0, WE[8])
        quantize_x(2)
        quantize_h(1)
        wres_q, wres_s = quantize_w("wres", wres_g)
        cast(LEAD)

        for s in range(STEPS):
            q, odd = s // 2, s % 2
            main(s, 0)
            if s >= 1:
                skip(s - 1)
            main(s, 1)
            if s + 2 < STEPS:
                hidden(s + 2)
            if s + 3 < STEPS:
                transposes(s + 3)
            if s + LEAD < STEPS:
                widen_gpsimd(s + LEAD)
            add_fut(s, 0)
            add_fut(s, 1)
            if s + 2 < STEPS:
                relu_h(s + 2)
            if s + 3 < STEPS:
                empty_x(s + 3)
            if s + LEAD + 1 < STEPS:
                cast(s + LEAD + 1)
            relu_z(s, 4 if s == STEPS - 1 else 1)
            if s >= 1:
                weigh_first(s - 1)
            if odd and q >= 1:
                weigh(q - 1, 2)
            if s + 3 < STEPS:
                quantize_both(s + 2)
            elif s + 2 < STEPS:
                quantize_h(s + 2)
            if q >= 1:
                weigh(q - 1, 3 if odd else 1)
            if odd and q >= 1:
                store(q - 1)
        last = STEPS // 2 - 1
        skip(STEPS - 1)
        for p in range(1, P_DEC):
            weigh(last, p, slice(0, 2))
        store(last, slice(0, 2))
        for i in range(2):
            weigh_first(STEPS - 1, slice(i, i + 1))
        for p in range(1, P_DEC):
            for i in range(2):
                weigh(last, p, slice(2 + i, 3 + i))
                if p == P_DEC - 1:
                    store(last, slice(2 + i, 3 + i))
